import numpy as np, ml_dtypes
CORES = [8,11,14,16,19,22,24,27,30]
N = 9
import mx_ref
NC, G = 192, 4
CNT = [[0,0,0,0,68,0,0,92,32],[32,16,72,72,0,0,0,0,0],[0,24,0,124,0,8,36,0,0],[0,0,56,52,0,56,0,28,0],[48,0,0,0,0,92,52,0,0],[0,32,4,60,0,0,8,0,88],[8,60,0,0,76,0,0,12,36],[0,48,44,0,28,24,48,0,0],[60,40,44,0,48,0,0,0,0]]
OFF = [[sum(c[:e]) for e in range(N + 1)] for c in CNT]
TOT = [sum(c[e] for c in CNT) for e in range(N)]
C = np.float32(0.019)
BF = ml_dtypes.bfloat16
def cut(t, i, w=512):
    return t[:, w * i:w * i + w]
def tile(rs):
    return np.stack(rs, axis=2).reshape(128, -1).astype(BF)
def layer(w, X):
    out = []
    for i in range(G):
        for t in range(len(X)):
            p = mx_ref.matmul(mx_ref.quantize(cut(w, len(X) * i + t)), X[t])
            z = p if t == 0 else z + p
        out.append(z)
    return out
def act(Z):
    return [np.maximum(z, 0) * C for z in Z]
def setup_inputs(rng):
    def f(*shape):
        return mx_ref.flush((rng.standard_normal(shape, dtype=np.float32) * np.exp2(rng.integers(-2, 3, shape[:-1] + (1,)))).astype(BF))
    return {"x": f(N, 128, 4 * NC), "w1": f(N, 128, G * 512), "w2": f(N, 128, 512)}
def setup_inputs_blocks(rng):
    d = setup_inputs(rng)
    for k in ("x", "w1", "w2"): d[k] = mx_ref.spread(d[k], rng, 4)
    return d
def setup_inputs_wide(rng):
    d = setup_inputs(rng)
    for k in ("x", "w1", "w2"): d[k] = mx_ref.flush((d[k].astype(np.float32) * np.exp2(rng.integers(-8, 9, (N, 1, 1))).astype(np.float32)).astype(BF))
    return d
def setup_inputs_zeros(rng):
    d = setup_inputs(rng); v = d["x"].reshape(N, 128, -1, 4).copy()
    v[np.broadcast_to((rng.random((N, 1, v.shape[2], 1)) < 0.33), v.shape)] = 0
    d["x"] = v.reshape(d["x"].shape)
    return d
def reference(x, w1, w2):
    y = np.full((N, 128, max(TOT)), np.nan, np.float32)
    for e in range(N):
        t = np.concatenate([x[j][:, 4 * OFF[j][e]:4 * OFF[j][e + 1]] for j in range(N)], axis=1)
        y[e][:, :TOT[e]] = mx_ref.matmul(mx_ref.quantize(w2[e]), mx_ref.quantize(tile(act(layer(w1[e], [mx_ref.quantize(t)])))))
    return {"y": y}

@@ -1,0 +1,305 @@
+from concourse.bass import DstId, RemoteDMATransfer
+from concourse.mybir import dt, AluOpType, ActivationFunctionType
+
+SIM = 32
+NC = 192
+YW = 308
+LAND = 512
+CONST = 0.019
+
+FUSE = True
+LATE_W = False
+IDLE_RELAY = False
+ENG_OFF = 8
+ENG_ON = 8
+
+SCRATCH = {
+    "xt": ("sbuf", [128, 4 * NC], "bfloat16"),
+    "w1t": ("sbuf", [128, 2048], "bfloat16"),
+    "w2t": ("sbuf", [128, 512], "bfloat16"),
+    "qb": ("sbuf", [128, NC + LAND], "float8_e4m3fn_x4"),
+    "sb": ("sbuf", [128, NC + LAND], "uint8"),
+    "rq": ("sbuf", [128, NC], "float8_e4m3fn_x4"),
+    "rs": ("sbuf", [128, NC], "uint8"),
+    "qw1": ("sbuf", [128, 512], "float8_e4m3fn_x4"),
+    "sw1": ("sbuf", [128, 512], "uint8"),
+    "qw2": ("sbuf", [128, 128], "float8_e4m3fn_x4"),
+    "sw2": ("sbuf", [128, 128], "uint8"),
+    "z": ("psum", [128, 2048], "float32"),
+    "yp": ("psum", [128, 512], "float32"),
+    "h": ("sbuf", [128, 4 * YW], "bfloat16"),
+    "qh": ("sbuf", [128, YW], "float8_e4m3fn_x4"),
+    "sh": ("sbuf", [128, YW], "uint8"),
+    "ysb": ("sbuf", [128, YW], "float32"),
+}
+SEMAPHORES = ["xl", "wl", "qx", "qw", "arr", "rca", "rsa", "snt", "mm0", "mm1", "mm2", "mm3", "act", "qh", "my", "cp",
+              "st", "go"]
+
+
+def _bits(mask):
+    return [b for b in range(16) if (mask >> b) & 1]
+
+
+def _hops(topo, a, b):
+    ca, cb = topo.chip(a), topo.chip(b)
+    if ca == cb:
+        return 0
+    return 1 if (topo.mates(ca, cb) or topo.same_plane(ca, cb)) else 2
+
+
+def _width(items, lim):
+    least = max([it["n"] for it in items if it["kind"] == "relay"] + [0])
+    best = None
+    for w in sorted({-(-it["n"] // k) for it in items for k in (1, 2, 3)}):
+        w += w & 1
+        if w < least:
+            continue
+        k_off = sum(-(-it["n"] // w) for it in items if it["hops"])
+        k_on = sum(-(-it["n"] // w) for it in items if not it["hops"])
+        if k_off > lim or k_on > lim:
+            continue
+        cost = w * (2 * k_off + k_on) + 80 * (k_off + k_on)
+        if best is None or cost < best[0]:
+            best = (cost, w)
+    return best[1]
+
+
+def _calls(items):
+    items = sorted(items, key=lambda it: (it["kind"] != "relay", -it["hops"], -it["n"]))
+    if not FUSE:
+        return [(it["n"], [(it, 0, it["n"])]) for it in items]
+    w = _width(items, 4)
+    pieces = []
+    for it in items:
+        po = 0
+        while po < it["n"]:
+            m = min(w, it["n"] - po)
+            pieces.append((it, po, m))
+            po += m
+    return [(w, pieces)]
+
+
+def _masks(topo, src, group):
+    off = [t["dst"] for call in group for t in call if topo.chip(t["dst"]) != topo.chip(src)]
+    off_bits = _bits(topo.mask(src, off[0]))[:ENG_OFF] if off else []
+    for call in group:
+        for far in (True, False):
+            trs = [t for t in call if (topo.chip(t["dst"]) != topo.chip(src)) == far]
+            if not trs:
+                continue
+            if far:
+                bits = off_bits
+            else:
+                bits = [b for b in _bits(topo.mask(src, trs[0]["dst"])) if b not in off_bits]
+                bits = bits[-(ENG_ON if off else ENG_ON + ENG_OFF):]
+            cnt = [1] * len(trs)
+            grown = True
+            while grown:
+                grown = False
+                for i in range(len(trs)):
+                    if sum(cnt) + cnt[i] <= len(bits):
+                        cnt[i] *= 2
+                        grown = True
+            at = 0
+            for i in sorted(range(len(trs)), key=lambda i: -cnt[i]):
+                trs[i]["mask"] = sum(1 << b for b in bits[at:at + cnt[i]])
+                trs[i]["eng"] = cnt[i]
+                at += cnt[i]
+
+
+def _plan(T, topo):
+    cores = list(T.cores)
+    cnt = T.tables["CNT"]
+    n = len(cores)
+    tot = [sum(cnt[j][e] for j in range(n)) for e in range(n)]
+    boff = [[sum(cnt[i][e] for i in range(j)) for e in range(n)] for j in range(n)]
+    pos, loads = [], []
+    for j in range(n):
+        back = sum(cnt[j][:j + 1]) if cnt[j][j] else 0
+        back = back % NC
+        order = [e for e in range(n) if sum(cnt[j][:e]) >= back] + [e for e in range(n) if sum(cnt[j][:e]) < back]
+        p, c = {}, 0
+        for e in order:
+            p[e] = c
+            c += cnt[j][e]
+        pos.append(p)
+        loads.append([(0, back, NC - back)] + ([(NC - back, 0, back)] if back else []))
+
+    groups = {}
+    arrive = [[] for _ in range(n)]
+    room = {}
+    onward = {}
+
+    def relay_of(src, dst):
+        cand = [c for c in range(SIM)
+                if topo.chip(c) == topo.chip(src) and c != src and topo.may_write(c, dst)
+                and ((c in cores) != IDLE_RELAY)]
+        return sorted(cand, key=lambda c: (topo.die(c) != topo.die(src), c))[0]
+
+    def cut(src, phase, items, buf):
+        group = groups.setdefault((src, phase), [])
+        for w, pieces in _calls(items):
+            call = []
+            group.append(call)
+            for it, po, m in pieces:
+                if it["kind"] == "relay":
+                    r = it["dst"]
+                    at = room.get(r, 0)
+                    room[r] = at + w
+                    ws = min(it["start"], it["hi"] - w)
+                    call.append({"dst": r, "sbuf": buf, "scol": ws, "dbuf": "r", "dcol": at, "w": w})
+                    for e, s, k in it["runs"]:
+                        onward.setdefault(r, []).append(
+                            {"kind": "main", "e": e, "j": it["j"], "start": at + s - ws, "n": k, "dst": cores[e],
+                             "hops": _hops(topo, r, cores[e]), "lo": at, "hi": at + w})
+                else:
+                    tr = {"dst": it["dst"], "sbuf": buf, "dbuf": "t", "w": w}
+                    call.append(tr)
+                    arrive[it["e"]].append({"j": it["j"], "po": po, "m": m, "spos": it["start"] + po,
+                                            "lo": it["lo"], "hi": it["hi"], "w": w, "tr": tr})
+
+    for j in range(n):
+        items, far = [], {}
+        for e in sorted(range(n), key=lambda e: pos[j][e]):
+            if e == j or not cnt[j][e]:
+                continue
+            if topo.may_write(cores[j], cores[e]):
+                items.append({"kind": "main", "e": e, "j": j, "start": pos[j][e], "n": cnt[j][e], "dst": cores[e],
+                              "hops": _hops(topo, cores[j], cores[e]), "lo": 0, "hi": NC})
+            else:
+                runs = far.setdefault(relay_of(cores[j], cores[e]), [])
+                if runs and runs[-1]["start"] + runs[-1]["n"] == pos[j][e]:
+                    runs[-1]["n"] += cnt[j][e]
+                    runs[-1]["runs"].append((e, pos[j][e], cnt[j][e]))
+                else:
+                    runs.append({"kind": "relay", "j": j, "start": pos[j][e], "n": cnt[j][e], "hops": 0, "lo": 0,
+                                 "hi": NC, "runs": [(e, pos[j][e], cnt[j][e])]})
+        for r in far:
+            for it in far[r]:
+                it["dst"] = r
+                items.append(it)
+        cut(cores[j], 0, items, "t")
+    for r in sorted(onward):
+        cut(r, 1, onward[r], "r")
+
+    view, segs = [], []
+    for e in range(n):
+        own = cnt[e][e]
+        lst = sorted(arrive[e], key=lambda a: ((a["j"] < e) if own else False, a["j"], a["po"]))
+        col, touch = NC, bool(own)
+        sg = [[NC - own, own, boff[e][e]]] if own else []
+        for a in lst:
+            lo_ws, hi_ws = max(a["lo"], a["spos"] + a["m"] - a["w"]), min(a["spos"], a["hi"] - a["w"])
+            ws = hi_ws if touch else lo_ws
+            a["tr"]["scol"], a["tr"]["dcol"] = ws, col
+            at, b = col + a["spos"] - ws, boff[a["j"]][e] + a["po"]
+            if sg and sg[-1][0] + sg[-1][1] == at and sg[-1][2] + sg[-1][1] == b:
+                sg[-1][1] += a["m"]
+            else:
+                sg.append([at, a["m"], b])
+            touch = (a["spos"] - ws + a["m"] == a["w"])
+            col += a["w"]
+        view.append((NC - own, col))
+        segs.append(sg)
+
+    for (src, _), group in groups.items():
+        _masks(topo, src, group)
+    got = {}
+    for (src, _), group in groups.items():
+        for call in group:
+            for t in call:
+                got[(t["dst"], t["dbuf"])] = got.get((t["dst"], t["dbuf"]), 0) + t["eng"]
+                got[(src, "s")] = got.get((src, "s"), 0) + 2 * t["eng"]
+    return {"tot": tot, "loads": loads, "groups": groups, "view": view, "segs": segs, "got": got}
+
+
+def _issue(g, T, topo, call, plane):
+    trs = []
+    for t in call:
+        rid, pid, _ = topo.addr(t["dst"])
+        sb = {"t": (T.qb, T.sb), "r": (T.rq, T.rs)}[t["sbuf"]][plane]
+        db = {"t": (T.qb, T.sb), "r": (T.rq, T.rs)}[t["dbuf"]][plane]
+        src = sb[:, t["scol"]:t["scol"] + t["w"]]
+        dst = db[:, t["dcol"]:t["dcol"] + t["w"]]
+        if plane == 0:
+            src, dst = src.bitcast(dt.uint8), dst.bitcast(dt.uint8)
+        sem = T.sem.arr if t["dbuf"] == "t" else (T.sem.rca, T.sem.rsa)[plane]
+        trs.append(RemoteDMATransfer(dst_ids=[DstId(rid=rid, pnc=pid)], dma_engine_mask=t["mask"], remote_sem=sem,
+                                     src=src, dst=dst))
+    g.remote_dma_fused(trs, local_sem=T.sem.snt)
+
+
+def rank_program(g, core, T, topo):
+    P = _plan(T, topo)
+    S = T.sem
+    rank = T.rank_of(core)
+    own_calls = P["groups"].get((core, 0), [])
+    fwd_calls = P["groups"].get((core, 1), [])
+
+    if own_calls:
+        g.wait_ge(S.qx, 1)
+        for call in own_calls:
+            _issue(g, T, topo, call, 0)
+            _issue(g, T, topo, call, 1)
+        if LATE_W:
+            g.sem_inc(S.go, 2)
+    if fwd_calls:
+        need = P["got"][(core, "r")]
+        g.wait_ge(S.rca, need)
+        for call in fwd_calls:
+            _issue(g, T, topo, call, 0)
+        g.wait_ge(S.rsa, need)
+        for call in fwd_calls:
+            _issue(g, T, topo, call, 1)
+    if own_calls or fwd_calls:
+        g.wait_ge(S.snt, P["got"][(core, "s")])
+    if rank is None:
+        return
+
+    tot = P["tot"][rank]
+    v0, v1 = P["view"][rank]
+    nv = v1 - v0
+    segs = P["segs"][rank]
+    vec, sca, ten, syn = g.vector, g.scalar, g.tensor, g.sync
+
+    for i, (tc, xc, w) in enumerate(P["loads"][rank]):
+        (syn, sca)[i % 2].dma_start(T.xt[:, 4 * tc:4 * (tc + w)], T.x[:, 4 * xc:4 * (xc + w)]).then_inc(S.xl, 16)
+    if LATE_W:
+        sca.wait_ge(S.go, 2)
+        syn.wait_ge(S.go, 2)
+    sca.dma_start(T.w1t[:], T.w1[:]).then_inc(S.wl, 16)
+    syn.dma_start(T.w2t[:], T.w2[:]).then_inc(S.wl, 16)
+
+    vec.wait_ge(S.xl, 16 * len(P["loads"][rank]))
+    vec.quantize_mx(T.qb[:, 0:NC], T.sb[:, 0:NC], T.xt[:]).then_inc(S.qx, 1)
+    vec.wait_ge(S.wl, 32)
+    vec.quantize_mx(T.qw1[:], T.sw1[:], T.w1t[:]).then_inc(S.qw, 1)
+    vec.quantize_mx(T.qw2[:], T.sw2[:], T.w2t[:]).then_inc(S.qw, 1)
+
+    ten.wait_ge(S.qw, 2)
+    ten.wait_ge(S.qx, 1)
+    ten.wait_ge(S.arr, 2 * P["got"][(core, "t")])
+    for b in range(4):
+        ten.matmul_mx(T.z[:, 512 * b:512 * b + nv], T.qw1[:, 128 * b:128 * b + 128], T.sw1[:, 128 * b:128 * b + 128],
+                      T.qb[:, v0:v1], T.sb[:, v0:v1], True, True).then_inc(S["mm%d" % b], 1)
+
+    for b in range(4):
+        q = (vec, sca)[b % 2]
+        q.wait_ge(S["mm%d" % b], 1)
+        for at, m, bo in segs:
+            src = T.z[:, 512 * b + at - v0:512 * b + at - v0 + m]
+            dst = T.h[:, 4 * bo + b:4 * (bo + m):4]
+            if b % 2 == 0:
+                vec.tensor_scalar(dst, src, 0.0, CONST, AluOpType.max, AluOpType.mult).then_inc(S.act, 1)
+            else:
+                sca.activation(dst, src, ActivationFunctionType.Relu, scale=CONST).then_inc(S.act, 1)
+
+    vec.wait_ge(S.act, 4 * len(segs))
+    vec.quantize_mx(T.qh[:, 0:tot], T.sh[:, 0:tot], T.h[:, 0:4 * tot]).then_inc(S.qh, 1)
+    ten.wait_ge(S.qh, 1)
+    ten.matmul_mx(T.yp[:, 0:tot], T.qw2[:], T.sw2[:], T.qh[:, 0:tot], T.sh[:, 0:tot], True, True).then_inc(S.my, 1)
+    vec.wait_ge(S.my, 1)
+    vec.tensor_copy(T.ysb[:, 0:tot], T.yp[:, 0:tot]).then_inc(S.cp, 1)
+    syn.wait_ge(S.cp, 1)
+    syn.dma_start(T.y[:, 0:tot], T.ysb[:, 0:tot]).then_inc(S.st, 16)
+    syn.wait_ge(S.st, 16)

@@ -1,17 +1,12 @@
 from concourse.bass import DstId, RemoteDMATransfer
 from concourse.mybir import dt, AluOpType, ActivationFunctionType
 
-SIM = 32
 NC = 192
 YW = 308
 LAND = 512
+LEAST = 128
 CONST = 0.019
-
-FUSE = True
-LATE_W = False
-IDLE_RELAY = False
-ENG_OFF = 8
-ENG_ON = 8
+EARLY = 64
 
 SCRATCH = {
     "xt": ("sbuf", [128, 4 * NC], "bfloat16"),
@@ -25,19 +20,18 @@ SCRATCH = {
     "sw1": ("sbuf", [128, 512], "uint8"),
     "qw2": ("sbuf", [128, 128], "float8_e4m3fn_x4"),
     "sw2": ("sbuf", [128, 128], "uint8"),
-    "z": ("psum", [128, 2048], "float32"),
-    "yp": ("psum", [128, 512], "float32"),
-    "h": ("sbuf", [128, 4 * YW], "bfloat16"),
-    "qh": ("sbuf", [128, YW], "float8_e4m3fn_x4"),
-    "sh": ("sbuf", [128, YW], "uint8"),
+    "z": ("psum", [128, 4096], "float32"),
+    "h0": ("sbuf", [128, 2048], "bfloat16"),
+    "h1": ("sbuf", [128, 2048], "bfloat16"),
+    "qh0": ("sbuf", [128, 512], "float8_e4m3fn_x4"),
+    "qh1": ("sbuf", [128, 512], "float8_e4m3fn_x4"),
+    "sh0": ("sbuf", [128, 512], "uint8"),
+    "sh1": ("sbuf", [128, 512], "uint8"),
     "ysb": ("sbuf", [128, YW], "float32"),
 }
-SEMAPHORES = ["xl", "wl", "qx", "qw", "arr", "rca", "rsa", "snt", "mm0", "mm1", "mm2", "mm3", "act", "qh", "my", "cp",
-              "st", "go"]
-
-
-def _bits(mask):
-    return [b for b in range(16) if (mask >> b) & 1]
+SEMAPHORES = ["xl", "w1l", "w2l", "qx", "qa0", "qa1", "qa2", "qa3", "qb2", "arr0", "arr1", "rca", "rsa", "snt",
+              "mm0", "mm1", "mm2", "mm3", "mm4", "mm5", "mm6", "mm7", "act0", "act1", "qh0", "qh1", "my0", "my1",
+              "cp", "st"]
 
 
 def _hops(topo, a, b):
@@ -45,66 +39,6 @@ def _hops(topo, a, b):
     if ca == cb:
         return 0
     return 1 if (topo.mates(ca, cb) or topo.same_plane(ca, cb)) else 2
-
-
-def _width(items, lim):
-    least = max([it["n"] for it in items if it["kind"] == "relay"] + [0])
-    best = None
-    for w in sorted({-(-it["n"] // k) for it in items for k in (1, 2, 3)}):
-        w += w & 1
-        if w < least:
-            continue
-        k_off = sum(-(-it["n"] // w) for it in items if it["hops"])
-        k_on = sum(-(-it["n"] // w) for it in items if not it["hops"])
-        if k_off > lim or k_on > lim:
-            continue
-        cost = w * (2 * k_off + k_on) + 80 * (k_off + k_on)
-        if best is None or cost < best[0]:
-            best = (cost, w)
-    return best[1]
-
-
-def _calls(items):
-    items = sorted(items, key=lambda it: (it["kind"] != "relay", -it["hops"], -it["n"]))
-    if not FUSE:
-        return [(it["n"], [(it, 0, it["n"])]) for it in items]
-    w = _width(items, 4)
-    pieces = []
-    for it in items:
-        po = 0
-        while po < it["n"]:
-            m = min(w, it["n"] - po)
-            pieces.append((it, po, m))
-            po += m
-    return [(w, pieces)]
-
-
-def _masks(topo, src, group):
-    off = [t["dst"] for call in group for t in call if topo.chip(t["dst"]) != topo.chip(src)]
-    off_bits = _bits(topo.mask(src, off[0]))[:ENG_OFF] if off else []
-    for call in group:
-        for far in (True, False):
-            trs = [t for t in call if (topo.chip(t["dst"]) != topo.chip(src)) == far]
-            if not trs:
-                continue
-            if far:
-                bits = off_bits
-            else:
-                bits = [b for b in _bits(topo.mask(src, trs[0]["dst"])) if b not in off_bits]
-                bits = bits[-(ENG_ON if off else ENG_ON + ENG_OFF):]
-            cnt = [1] * len(trs)
-            grown = True
-            while grown:
-                grown = False
-                for i in range(len(trs)):
-                    if sum(cnt) + cnt[i] <= len(bits):
-                        cnt[i] *= 2
-                        grown = True
-            at = 0
-            for i in sorted(range(len(trs)), key=lambda i: -cnt[i]):
-                trs[i]["mask"] = sum(1 << b for b in bits[at:at + cnt[i]])
-                trs[i]["eng"] = cnt[i]
-                at += cnt[i]
 
 
 def _plan(T, topo):
@@ -125,38 +59,52 @@ def _plan(T, topo):
         pos.append(p)
         loads.append([(0, back, NC - back)] + ([(NC - back, 0, back)] if back else []))
 
-    groups = {}
+    late = {}
+    for e in range(n):
+        way = {j: (_hops(topo, cores[j], cores[e]) if topo.may_write(cores[j], cores[e]) else 3)
+               for j in range(n) if j != e and cnt[j][e]}
+        top = max(way.values())
+        lt = [j for j in way if way[j] == top]
+        size = sum(cnt[j][e] for j in lt)
+        for j in sorted([j for j in way if 0 < way[j] < top], key=lambda j: (-way[j], cnt[j][e])):
+            if size + cnt[j][e] <= LEAST:
+                lt.append(j)
+                size += cnt[j][e]
+        if tot[e] - size < EARLY:
+            lt = list(way)
+        for j in way:
+            late[(j, e)] = j in lt
+
+    sends = {}
     arrive = [[] for _ in range(n)]
     room = {}
     onward = {}
 
     def relay_of(src, dst):
-        cand = [c for c in range(SIM)
-                if topo.chip(c) == topo.chip(src) and c != src and topo.may_write(c, dst)
-                and ((c in cores) != IDLE_RELAY)]
+        cand = [c for c in cores if topo.chip(c) == topo.chip(src) and c != src and topo.may_write(c, dst)]
         return sorted(cand, key=lambda c: (topo.die(c) != topo.die(src), c))[0]
 
     def cut(src, phase, items, buf):
-        group = groups.setdefault((src, phase), [])
-        for w, pieces in _calls(items):
-            call = []
-            group.append(call)
-            for it, po, m in pieces:
-                if it["kind"] == "relay":
-                    r = it["dst"]
-                    at = room.get(r, 0)
-                    room[r] = at + w
-                    ws = min(it["start"], it["hi"] - w)
-                    call.append({"dst": r, "sbuf": buf, "scol": ws, "dbuf": "r", "dcol": at, "w": w})
-                    for e, s, k in it["runs"]:
-                        onward.setdefault(r, []).append(
-                            {"kind": "main", "e": e, "j": it["j"], "start": at + s - ws, "n": k, "dst": cores[e],
-                             "hops": _hops(topo, r, cores[e]), "lo": at, "hi": at + w})
-                else:
-                    tr = {"dst": it["dst"], "sbuf": buf, "dbuf": "t", "w": w}
-                    call.append(tr)
-                    arrive[it["e"]].append({"j": it["j"], "po": po, "m": m, "spos": it["start"] + po,
-                                            "lo": it["lo"], "hi": it["hi"], "w": w, "tr": tr})
+        items = sorted(items, key=lambda it: (it["kind"] != "relay", it["hops"] < 2, it["late"], -it["n"]))
+        far = [it["dst"] for it in items if it["hops"]]
+        away = topo.mask(src, far[0]) if far else 0
+        for it in items:
+            mask = away if it["hops"] else topo.mask(src, it["dst"]) & ~away
+            tr = {"dst": it["dst"], "sbuf": buf, "scol": it["start"], "w": it["n"], "mask": mask,
+                  "eng": bin(mask).count("1")}
+            sends.setdefault((src, phase), []).append(tr)
+            if it["kind"] == "relay":
+                r = it["dst"]
+                at = room.get(r, 0)
+                room[r] = at + it["n"]
+                tr["dbuf"], tr["dcol"], tr["sem"] = "r", at, "r"
+                for e, s, k in it["runs"]:
+                    onward.setdefault(r, []).append(
+                        {"kind": "main", "e": e, "j": it["j"], "start": at + s - it["start"], "n": k, "dst": cores[e],
+                         "hops": _hops(topo, r, cores[e]), "late": True})
+            else:
+                tr["dbuf"] = "t"
+                arrive[it["e"]].append({"j": it["j"], "m": it["n"], "tr": tr})
 
     for j in range(n):
         items, far = [], {}
@@ -165,15 +113,15 @@ def _plan(T, topo):
                 continue
             if topo.may_write(cores[j], cores[e]):
                 items.append({"kind": "main", "e": e, "j": j, "start": pos[j][e], "n": cnt[j][e], "dst": cores[e],
-                              "hops": _hops(topo, cores[j], cores[e]), "lo": 0, "hi": NC})
+                              "hops": _hops(topo, cores[j], cores[e]), "late": late[(j, e)]})
             else:
                 runs = far.setdefault(relay_of(cores[j], cores[e]), [])
                 if runs and runs[-1]["start"] + runs[-1]["n"] == pos[j][e]:
                     runs[-1]["n"] += cnt[j][e]
                     runs[-1]["runs"].append((e, pos[j][e], cnt[j][e]))
                 else:
-                    runs.append({"kind": "relay", "j": j, "start": pos[j][e], "n": cnt[j][e], "hops": 0, "lo": 0,
-                                 "hi": NC, "runs": [(e, pos[j][e], cnt[j][e])]})
+                    runs.append({"kind": "relay", "j": j, "start": pos[j][e], "n": cnt[j][e], "hops": 0,
+                                 "late": False, "runs": [(e, pos[j][e], cnt[j][e])]})
         for r in far:
             for it in far[r]:
                 it["dst"] = r
@@ -182,124 +130,133 @@ def _plan(T, topo):
     for r in sorted(onward):
         cut(r, 1, onward[r], "r")
 
-    view, segs = [], []
+    stages = []
     for e in range(n):
         own = cnt[e][e]
-        lst = sorted(arrive[e], key=lambda a: ((a["j"] < e) if own else False, a["j"], a["po"]))
-        col, touch = NC, bool(own)
-        sg = [[NC - own, own, boff[e][e]]] if own else []
-        for a in lst:
-            lo_ws, hi_ws = max(a["lo"], a["spos"] + a["m"] - a["w"]), min(a["spos"], a["hi"] - a["w"])
-            ws = hi_ws if touch else lo_ws
-            a["tr"]["scol"], a["tr"]["dcol"] = ws, col
-            at, b = col + a["spos"] - ws, boff[a["j"]][e] + a["po"]
-            if sg and sg[-1][0] + sg[-1][1] == at and sg[-1][2] + sg[-1][1] == b:
-                sg[-1][1] += a["m"]
-            else:
-                sg.append([at, a["m"], b])
-            touch = (a["spos"] - ws + a["m"] == a["w"])
-            col += a["w"]
-        view.append((NC - own, col))
-        segs.append(sg)
+        col, sts = NC, []
+        for lt in (False, True):
+            lst = sorted([a for a in arrive[e] if late[(a["j"], e)] == lt],
+                         key=lambda a: ((a["j"] < e) if own else False, a["j"]))
+            mine = own if not sts else 0
+            if not lst and not (mine and not lt):
+                continue
+            first = col - mine
+            sg = [[NC - own, own, boff[e][e]]] if mine else []
+            for a in lst:
+                a["tr"]["dcol"], a["tr"]["sem"] = col, "arr%d" % lt
+                b = boff[a["j"]][e]
+                if sg and sg[-1][0] + sg[-1][1] == col and sg[-1][2] + sg[-1][1] == b:
+                    sg[-1][1] += a["m"]
+                else:
+                    sg.append([col, a["m"], b])
+                col += a["m"]
+            sts.append({"v0": min(first, col - LEAST), "v1": col, "segs": sg, "sem": "arr%d" % lt, "any": bool(lst)})
+        stages.append(sts)
 
-    for (src, _), group in groups.items():
-        _masks(topo, src, group)
     got = {}
-    for (src, _), group in groups.items():
-        for call in group:
-            for t in call:
-                got[(t["dst"], t["dbuf"])] = got.get((t["dst"], t["dbuf"]), 0) + t["eng"]
-                got[(src, "s")] = got.get((src, "s"), 0) + 2 * t["eng"]
-    return {"tot": tot, "loads": loads, "groups": groups, "view": view, "segs": segs, "got": got}
+    for (src, _), lst in sends.items():
+        for t in lst:
+            got[(t["dst"], t["sem"])] = got.get((t["dst"], t["sem"]), 0) + t["eng"]
+            got[(src, "s")] = got.get((src, "s"), 0) + 2 * t["eng"]
+    return {"tot": tot, "loads": loads, "sends": sends, "stages": stages, "got": got}
 
 
-def _issue(g, T, topo, call, plane):
-    trs = []
-    for t in call:
-        rid, pid, _ = topo.addr(t["dst"])
-        sb = {"t": (T.qb, T.sb), "r": (T.rq, T.rs)}[t["sbuf"]][plane]
-        db = {"t": (T.qb, T.sb), "r": (T.rq, T.rs)}[t["dbuf"]][plane]
-        src = sb[:, t["scol"]:t["scol"] + t["w"]]
-        dst = db[:, t["dcol"]:t["dcol"] + t["w"]]
-        if plane == 0:
-            src, dst = src.bitcast(dt.uint8), dst.bitcast(dt.uint8)
-        sem = T.sem.arr if t["dbuf"] == "t" else (T.sem.rca, T.sem.rsa)[plane]
-        trs.append(RemoteDMATransfer(dst_ids=[DstId(rid=rid, pnc=pid)], dma_engine_mask=t["mask"], remote_sem=sem,
-                                     src=src, dst=dst))
-    g.remote_dma_fused(trs, local_sem=T.sem.snt)
+def _issue(g, T, topo, t, plane):
+    rid, pid, _ = topo.addr(t["dst"])
+    sb = {"t": (T.qb, T.sb), "r": (T.rq, T.rs)}[t["sbuf"]][plane]
+    db = {"t": (T.qb, T.sb), "r": (T.rq, T.rs)}[t["dbuf"]][plane]
+    src = sb[:, t["scol"]:t["scol"] + t["w"]]
+    dst = db[:, t["dcol"]:t["dcol"] + t["w"]]
+    if plane == 0:
+        src, dst = src.bitcast(dt.uint8), dst.bitcast(dt.uint8)
+    sem = T.sem[t["sem"]] if t["dbuf"] == "t" else (T.sem.rca, T.sem.rsa)[plane]
+    g.remote_dma_fused([RemoteDMATransfer(dst_ids=[DstId(rid=rid, pnc=pid)], dma_engine_mask=t["mask"],
+                                          remote_sem=sem, src=src, dst=dst)], local_sem=T.sem.snt)
 
 
 def rank_program(g, core, T, topo):
-    P = _plan(T, topo)
-    S = T.sem
     rank = T.rank_of(core)
-    own_calls = P["groups"].get((core, 0), [])
-    fwd_calls = P["groups"].get((core, 1), [])
-
-    if own_calls:
-        g.wait_ge(S.qx, 1)
-        for call in own_calls:
-            _issue(g, T, topo, call, 0)
-            _issue(g, T, topo, call, 1)
-        if LATE_W:
-            g.sem_inc(S.go, 2)
-    if fwd_calls:
-        need = P["got"][(core, "r")]
-        g.wait_ge(S.rca, need)
-        for call in fwd_calls:
-            _issue(g, T, topo, call, 0)
-        g.wait_ge(S.rsa, need)
-        for call in fwd_calls:
-            _issue(g, T, topo, call, 1)
-    if own_calls or fwd_calls:
-        g.wait_ge(S.snt, P["got"][(core, "s")])
     if rank is None:
         return
+    P = _plan(T, topo)
+    S = T.sem
+    own_sends = P["sends"].get((core, 0), [])
+    fwd_sends = P["sends"].get((core, 1), [])
+
+    g.wait_ge(S.qx, 1)
+    for t in own_sends:
+        _issue(g, T, topo, t, 0)
+        _issue(g, T, topo, t, 1)
+    if fwd_sends:
+        need = P["got"][(core, "r")]
+        g.wait_ge(S.rca, need)
+        for t in fwd_sends:
+            _issue(g, T, topo, t, 0)
+        g.wait_ge(S.rsa, need)
+        for t in fwd_sends:
+            _issue(g, T, topo, t, 1)
+    g.wait_ge(S.snt, P["got"][(core, "s")])
 
     tot = P["tot"][rank]
-    v0, v1 = P["view"][rank]
-    nv = v1 - v0
-    segs = P["segs"][rank]
+    stages = P["stages"][rank]
     vec, sca, ten, syn = g.vector, g.scalar, g.tensor, g.sync
 
-    for i, (tc, xc, w) in enumerate(P["loads"][rank]):
-        (syn, sca)[i % 2].dma_start(T.xt[:, 4 * tc:4 * (tc + w)], T.x[:, 4 * xc:4 * (xc + w)]).then_inc(S.xl, 16)
-    if LATE_W:
-        sca.wait_ge(S.go, 2)
-        syn.wait_ge(S.go, 2)
-    sca.dma_start(T.w1t[:], T.w1[:]).then_inc(S.wl, 16)
-    syn.dma_start(T.w2t[:], T.w2[:]).then_inc(S.wl, 16)
+    for tc, xc, w in P["loads"][rank]:
+        syn.dma_start(T.xt[:, 4 * tc:4 * (tc + w)], T.x[:, 4 * xc:4 * (xc + w)]).then_inc(S.xl, 16)
+    syn.dma_start(T.w1t[:], T.w1[:]).then_inc(S.w1l, 16)
+    syn.dma_start(T.w2t[:], T.w2[:]).then_inc(S.w2l, 16)
 
     vec.wait_ge(S.xl, 16 * len(P["loads"][rank]))
     vec.quantize_mx(T.qb[:, 0:NC], T.sb[:, 0:NC], T.xt[:]).then_inc(S.qx, 1)
-    vec.wait_ge(S.wl, 32)
-    vec.quantize_mx(T.qw1[:], T.sw1[:], T.w1t[:]).then_inc(S.qw, 1)
-    vec.quantize_mx(T.qw2[:], T.sw2[:], T.w2t[:]).then_inc(S.qw, 1)
+    vec.wait_ge(S.w1l, 16)
+    for b in range(4):
+        vec.quantize_mx(T.qw1[:, 128 * b:128 * b + 128], T.sw1[:, 128 * b:128 * b + 128],
+                        T.w1t[:, 512 * b:512 * b + 512]).then_inc(S["qa%d" % b], 1)
+    vec.wait_ge(S.w2l, 16)
+    vec.quantize_mx(T.qw2[:], T.sw2[:], T.w2t[:]).then_inc(S.qb2, 1)
 
-    ten.wait_ge(S.qw, 2)
     ten.wait_ge(S.qx, 1)
-    ten.wait_ge(S.arr, 2 * P["got"][(core, "t")])
-    for b in range(4):
-        ten.matmul_mx(T.z[:, 512 * b:512 * b + nv], T.qw1[:, 128 * b:128 * b + 128], T.sw1[:, 128 * b:128 * b + 128],
-                      T.qb[:, v0:v1], T.sb[:, v0:v1], True, True).then_inc(S["mm%d" % b], 1)
-
-    for b in range(4):
-        q = (vec, sca)[b % 2]
-        q.wait_ge(S["mm%d" % b], 1)
-        for at, m, bo in segs:
-            src = T.z[:, 512 * b + at - v0:512 * b + at - v0 + m]
-            dst = T.h[:, 4 * bo + b:4 * (bo + m):4]
+    for k, st in enumerate(stages):
+        v0, v1 = st["v0"], st["v1"]
+        nv = v1 - v0
+        if st["any"]:
+            ten.wait_ge(S[st["sem"]], 2 * P["got"][(core, st["sem"])])
+        for b in range(4):
+            c = 512 * (4 * k + b)
+            if k == 0:
+                ten.wait_ge(S["qa%d" % b], 1)
+            ten.matmul_mx(T.z[:, c:c + nv], T.qw1[:, 128 * b:128 * b + 128], T.sw1[:, 128 * b:128 * b + 128],
+                          T.qb[:, v0:v1], T.sb[:, v0:v1], True, True).then_inc(S["mm%d" % (4 * k + b)], 1)
+            q = (vec, sca)[b % 2]
+            q.wait_ge(S["mm%d" % (4 * k + b)], 1)
+            dst = T["h%d" % k][:, b:4 * nv:4]
             if b % 2 == 0:
-                vec.tensor_scalar(dst, src, 0.0, CONST, AluOpType.max, AluOpType.mult).then_inc(S.act, 1)
+                vec.tensor_scalar(dst, T.z[:, c:c + nv], 0.0, CONST, AluOpType.max, AluOpType.mult).then_inc(
+                    S["act%d" % k], 1)
             else:
-                sca.activation(dst, src, ActivationFunctionType.Relu, scale=CONST).then_inc(S.act, 1)
+                sca.activation(dst, T.z[:, c:c + nv], ActivationFunctionType.Relu, scale=CONST).then_inc(
+                    S["act%d" % k], 1)
+        vec.wait_ge(S["act%d" % k], 4)
+        vec.quantize_mx(T["qh%d" % k][:, 0:nv], T["sh%d" % k][:, 0:nv], T["h%d" % k][:, 0:4 * nv]).then_inc(
+            S["qh%d" % k], 1)
 
-    vec.wait_ge(S.act, 4 * len(segs))
-    vec.quantize_mx(T.qh[:, 0:tot], T.sh[:, 0:tot], T.h[:, 0:4 * tot]).then_inc(S.qh, 1)
-    ten.wait_ge(S.qh, 1)
-    ten.matmul_mx(T.yp[:, 0:tot], T.qw2[:], T.sw2[:], T.qh[:, 0:tot], T.sh[:, 0:tot], True, True).then_inc(S.my, 1)
-    vec.wait_ge(S.my, 1)
-    vec.tensor_copy(T.ysb[:, 0:tot], T.yp[:, 0:tot]).then_inc(S.cp, 1)
-    syn.wait_ge(S.cp, 1)
+    ncp = 0
+    ten.wait_ge(S.qb2, 1)
+    for k, st in enumerate(stages):
+        v0, v1 = st["v0"], st["v1"]
+        nv = v1 - v0
+        ten.wait_ge(S["qh%d" % k], 1)
+        ten.matmul_mx(T.z[:, 512 * k:512 * k + nv], T.qw2[:], T.sw2[:], T["qh%d" % k][:, 0:nv], T["sh%d" % k][:, 0:nv],
+                      True, True).then_inc(S["my%d" % k], 1)
+        last = k == len(stages) - 1
+        (vec if last else sca).wait_ge(S["my%d" % k], 1)
+        for at, m, bo in st["segs"]:
+            src = T.z[:, 512 * k + at - v0:512 * k + at - v0 + m]
+            if last:
+                vec.tensor_copy(T.ysb[:, bo:bo + m], src).then_inc(S.cp, 1)
+            else:
+                sca.activation(T.ysb[:, bo:bo + m], src, ActivationFunctionType.Copy).then_inc(S.cp, 1)
+            ncp += 1
+    syn.wait_ge(S.cp, ncp)
     syn.dma_start(T.y[:, 0:tot], T.ysb[:, 0:tot]).then_inc(S.st, 16)
     syn.wait_ge(S.st, 16)

from concourse.bass import DstId, RemoteDMATransfer
from concourse.mybir import dt, AluOpType, ActivationFunctionType

NC = 192
YW = 308
LAND = 512
LEAST = 128
CONST = 0.019
EARLY = 64

SCRATCH = {
    "xt": ("sbuf", [128, 4 * NC], "bfloat16"),
    "w1t": ("sbuf", [128, 2048], "bfloat16"),
    "w2t": ("sbuf", [128, 512], "bfloat16"),
    "qb": ("sbuf", [128, NC + LAND], "float8_e4m3fn_x4"),
    "sb": ("sbuf", [128, NC + LAND], "uint8"),
    "rq": ("sbuf", [128, NC], "float8_e4m3fn_x4"),
    "rs": ("sbuf", [128, NC], "uint8"),
    "qw1": ("sbuf", [128, 512], "float8_e4m3fn_x4"),
    "sw1": ("sbuf", [128, 512], "uint8"),
    "qw2": ("sbuf", [128, 128], "float8_e4m3fn_x4"),
    "sw2": ("sbuf", [128, 128], "uint8"),
    "z": ("psum", [128, 4096], "float32"),
    "h0": ("sbuf", [128, 2048], "bfloat16"),
    "h1": ("sbuf", [128, 2048], "bfloat16"),
    "qh0": ("sbuf", [128, 512], "float8_e4m3fn_x4"),
    "qh1": ("sbuf", [128, 512], "float8_e4m3fn_x4"),
    "sh0": ("sbuf", [128, 512], "uint8"),
    "sh1": ("sbuf", [128, 512], "uint8"),
    "ysb": ("sbuf", [128, YW], "float32"),
}
SEMAPHORES = ["xl", "w1l", "w2l", "qx", "qa0", "qa1", "qa2", "qa3", "qb2", "arr0", "arr1", "rca", "rsa", "snt",
              "mm0", "mm1", "mm2", "mm3", "mm4", "mm5", "mm6", "mm7", "act0", "act1", "qh0", "qh1", "my0", "my1",
              "cp", "st"]


def _hops(topo, a, b):
    ca, cb = topo.chip(a), topo.chip(b)
    if ca == cb:
        return 0
    return 1 if (topo.mates(ca, cb) or topo.same_plane(ca, cb)) else 2


def _plan(T, topo):
    cores = list(T.cores)
    cnt = T.tables["CNT"]
    n = len(cores)
    tot = [sum(cnt[j][e] for j in range(n)) for e in range(n)]
    boff = [[sum(cnt[i][e] for i in range(j)) for e in range(n)] for j in range(n)]
    pos, loads = [], []
    for j in range(n):
        back = sum(cnt[j][:j + 1]) if cnt[j][j] else 0
        back = back % NC
        order = [e for e in range(n) if sum(cnt[j][:e]) >= back] + [e for e in range(n) if sum(cnt[j][:e]) < back]
        p, c = {}, 0
        for e in order:
            p[e] = c
            c += cnt[j][e]
        pos.append(p)
        loads.append([(0, back, NC - back)] + ([(NC - back, 0, back)] if back else []))

    late = {}
    for e in range(n):
        way = {j: (_hops(topo, cores[j], cores[e]) if topo.may_write(cores[j], cores[e]) else 3)
               for j in range(n) if j != e and cnt[j][e]}
        top = max(way.values())
        lt = [j for j in way if way[j] == top]
        size = sum(cnt[j][e] for j in lt)
        for j in sorted([j for j in way if 0 < way[j] < top], key=lambda j: (-way[j], cnt[j][e])):
            if size + cnt[j][e] <= LEAST:
                lt.append(j)
                size += cnt[j][e]
        if tot[e] - size < EARLY:
            lt = list(way)
        for j in way:
            late[(j, e)] = j in lt

    sends = {}
    arrive = [[] for _ in range(n)]
    room = {}
    onward = {}

    def relay_of(src, dst):
        cand = [c for c in cores if topo.chip(c) == topo.chip(src) and c != src and topo.may_write(c, dst)]
        return sorted(cand, key=lambda c: (topo.die(c) != topo.die(src), c))[0]

    def cut(src, phase, items, buf):
        items = sorted(items, key=lambda it: (it["kind"] != "relay", it["hops"] < 2, it["late"], -it["n"]))
        far = [it["dst"] for it in items if it["hops"]]
        away = topo.mask(src, far[0]) if far else 0
        for it in items:
            mask = away if it["hops"] else topo.mask(src, it["dst"]) & ~away
            tr = {"dst": it["dst"], "sbuf": buf, "scol": it["start"], "w": it["n"], "mask": mask,
                  "eng": bin(mask).count("1")}
            sends.setdefault((src, phase), []).append(tr)
            if it["kind"] == "relay":
                r = it["dst"]
                at = room.get(r, 0)
                room[r] = at + it["n"]
                tr["dbuf"], tr["dcol"], tr["sem"] = "r", at, "r"
                for e, s, k in it["runs"]:
                    onward.setdefault(r, []).append(
                        {"kind": "main", "e": e, "j": it["j"], "start": at + s - it["start"], "n": k, "dst": cores[e],
                         "hops": _hops(topo, r, cores[e]), "late": True})
            else:
                tr["dbuf"] = "t"
                arrive[it["e"]].append({"j": it["j"], "m": it["n"], "tr": tr})

    for j in range(n):
        items, far = [], {}
        for e in sorted(range(n), key=lambda e: pos[j][e]):
            if e == j or not cnt[j][e]:
                continue
            if topo.may_write(cores[j], cores[e]):
                items.append({"kind": "main", "e": e, "j": j, "start": pos[j][e], "n": cnt[j][e], "dst": cores[e],
                              "hops": _hops(topo, cores[j], cores[e]), "late": late[(j, e)]})
            else:
                runs = far.setdefault(relay_of(cores[j], cores[e]), [])
                if runs and runs[-1]["start"] + runs[-1]["n"] == pos[j][e]:
                    runs[-1]["n"] += cnt[j][e]
                    runs[-1]["runs"].append((e, pos[j][e], cnt[j][e]))
                else:
                    runs.append({"kind": "relay", "j": j, "start": pos[j][e], "n": cnt[j][e], "hops": 0,
                                 "late": False, "runs": [(e, pos[j][e], cnt[j][e])]})
        for r in far:
            for it in far[r]:
                it["dst"] = r
                items.append(it)
        cut(cores[j], 0, items, "t")
    for r in sorted(onward):
        cut(r, 1, onward[r], "r")

    stages = []
    for e in range(n):
        own = cnt[e][e]
        col, sts = NC, []
        for lt in (False, True):
            lst = sorted([a for a in arrive[e] if late[(a["j"], e)] == lt],
                         key=lambda a: ((a["j"] < e) if own else False, a["j"]))
            mine = own if not sts else 0
            if not lst and not (mine and not lt):
                continue
            first = col - mine
            sg = [[NC - own, own, boff[e][e]]] if mine else []
            for a in lst:
                a["tr"]["dcol"], a["tr"]["sem"] = col, "arr%d" % lt
                b = boff[a["j"]][e]
                if sg and sg[-1][0] + sg[-1][1] == col and sg[-1][2] + sg[-1][1] == b:
                    sg[-1][1] += a["m"]
                else:
                    sg.append([col, a["m"], b])
                col += a["m"]
            sts.append({"v0": min(first, col - LEAST), "v1": col, "segs": sg, "sem": "arr%d" % lt, "any": bool(lst)})
        stages.append(sts)

    got = {}
    for (src, _), lst in sends.items():
        for t in lst:
            got[(t["dst"], t["sem"])] = got.get((t["dst"], t["sem"]), 0) + t["eng"]
            got[(src, "s")] = got.get((src, "s"), 0) + 2 * t["eng"]
    return {"tot": tot, "loads": loads, "sends": sends, "stages": stages, "got": got}


def _issue(g, T, topo, t, plane):
    rid, pid, _ = topo.addr(t["dst"])
    sb = {"t": (T.qb, T.sb), "r": (T.rq, T.rs)}[t["sbuf"]][plane]
    db = {"t": (T.qb, T.sb), "r": (T.rq, T.rs)}[t["dbuf"]][plane]
    src = sb[:, t["scol"]:t["scol"] + t["w"]]
    dst = db[:, t["dcol"]:t["dcol"] + t["w"]]
    if plane == 0:
        src, dst = src.bitcast(dt.uint8), dst.bitcast(dt.uint8)
    sem = T.sem[t["sem"]] if t["dbuf"] == "t" else (T.sem.rca, T.sem.rsa)[plane]
    g.remote_dma_fused([RemoteDMATransfer(dst_ids=[DstId(rid=rid, pnc=pid)], dma_engine_mask=t["mask"],
                                          remote_sem=sem, src=src, dst=dst)], local_sem=T.sem.snt)


def rank_program(g, core, T, topo):
    rank = T.rank_of(core)
    if rank is None:
        return
    P = _plan(T, topo)
    S = T.sem
    own_sends = P["sends"].get((core, 0), [])
    fwd_sends = P["sends"].get((core, 1), [])

    g.wait_ge(S.qx, 1)
    for t in own_sends:
        _issue(g, T, topo, t, 0)
        _issue(g, T, topo, t, 1)
    if fwd_sends:
        need = P["got"][(core, "r")]
        g.wait_ge(S.rca, need)
        for t in fwd_sends:
            _issue(g, T, topo, t, 0)
        g.wait_ge(S.rsa, need)
        for t in fwd_sends:
            _issue(g, T, topo, t, 1)
    g.wait_ge(S.snt, P["got"][(core, "s")])

    tot = P["tot"][rank]
    stages = P["stages"][rank]
    vec, sca, ten, syn = g.vector, g.scalar, g.tensor, g.sync

    for tc, xc, w in P["loads"][rank]:
        syn.dma_start(T.xt[:, 4 * tc:4 * (tc + w)], T.x[:, 4 * xc:4 * (xc + w)]).then_inc(S.xl, 16)
    syn.dma_start(T.w1t[:], T.w1[:]).then_inc(S.w1l, 16)
    syn.dma_start(T.w2t[:], T.w2[:]).then_inc(S.w2l, 16)

    vec.wait_ge(S.xl, 16 * len(P["loads"][rank]))
    vec.quantize_mx(T.qb[:, 0:NC], T.sb[:, 0:NC], T.xt[:]).then_inc(S.qx, 1)
    vec.wait_ge(S.w1l, 16)
    for b in range(4):
        vec.quantize_mx(T.qw1[:, 128 * b:128 * b + 128], T.sw1[:, 128 * b:128 * b + 128],
                        T.w1t[:, 512 * b:512 * b + 512]).then_inc(S["qa%d" % b], 1)
    vec.wait_ge(S.w2l, 16)
    vec.quantize_mx(T.qw2[:], T.sw2[:], T.w2t[:]).then_inc(S.qb2, 1)

    ten.wait_ge(S.qx, 1)
    for k, st in enumerate(stages):
        v0, v1 = st["v0"], st["v1"]
        nv = v1 - v0
        if st["any"]:
            ten.wait_ge(S[st["sem"]], 2 * P["got"][(core, st["sem"])])
        for b in range(4):
            c = 512 * (4 * k + b)
            if k == 0:
                ten.wait_ge(S["qa%d" % b], 1)
            ten.matmul_mx(T.z[:, c:c + nv], T.qw1[:, 128 * b:128 * b + 128], T.sw1[:, 128 * b:128 * b + 128],
                          T.qb[:, v0:v1], T.sb[:, v0:v1], True, True).then_inc(S["mm%d" % (4 * k + b)], 1)
            q = (vec, sca)[b % 2]
            q.wait_ge(S["mm%d" % (4 * k + b)], 1)
            dst = T["h%d" % k][:, b:4 * nv:4]
            if b % 2 == 0:
                vec.tensor_scalar(dst, T.z[:, c:c + nv], 0.0, CONST, AluOpType.max, AluOpType.mult).then_inc(
                    S["act%d" % k], 1)
            else:
                sca.activation(dst, T.z[:, c:c + nv], ActivationFunctionType.Relu, scale=CONST).then_inc(
                    S["act%d" % k], 1)
        vec.wait_ge(S["act%d" % k], 4)
        vec.quantize_mx(T["qh%d" % k][:, 0:nv], T["sh%d" % k][:, 0:nv], T["h%d" % k][:, 0:4 * nv]).then_inc(
            S["qh%d" % k], 1)

    ncp = 0
    ten.wait_ge(S.qb2, 1)
    for k, st in enumerate(stages):
        v0, v1 = st["v0"], st["v1"]
        nv = v1 - v0
        ten.wait_ge(S["qh%d" % k], 1)
        ten.matmul_mx(T.z[:, 512 * k:512 * k + nv], T.qw2[:], T.sw2[:], T["qh%d" % k][:, 0:nv], T["sh%d" % k][:, 0:nv],
                      True, True).then_inc(S["my%d" % k], 1)
        last = k == len(stages) - 1
        (vec if last else sca).wait_ge(S["my%d" % k], 1)
        for at, m, bo in st["segs"]:
            src = T.z[:, 512 * k + at - v0:512 * k + at - v0 + m]
            if last:
                vec.tensor_copy(T.ysb[:, bo:bo + m], src).then_inc(S.cp, 1)
            else:
                sca.activation(T.ysb[:, bo:bo + m], src, ActivationFunctionType.Copy).then_inc(S.cp, 1)
            ncp += 1
    syn.wait_ge(S.cp, ncp)
    syn.dma_start(T.y[:, 0:tot], T.ysb[:, 0:tot]).then_inc(S.st, 16)
    syn.wait_ge(S.st, 16)
